import numpy as np
import ml_dtypes


def mxq(x, axis, fmt="e4m3"):
    dtype, down = {"e4m3": (ml_dtypes.float8_e4m3fn, 7), "e5m2": (ml_dtypes.float8_e5m2, 14)}[fmt]
    v = np.moveaxis(np.asarray(x, np.float32).astype(ml_dtypes.bfloat16).astype(np.float64), axis, -1)
    blocks = v.reshape(v.shape[:-1] + (-1, 32))
    amax = np.abs(blocks).max(-1, keepdims=True)
    byte = np.maximum(np.where(amax > 0, np.frexp(amax)[1] - 1 + 127, 0) - down, 1)
    scale = np.exp2(byte - 127.0)
    codes = (blocks / scale).astype(np.float32).astype(dtype).astype(np.float64)
    return np.moveaxis((codes * scale).reshape(v.shape), -1, axis)


WIDE = False


def mx_kscale(k):
    if not WIDE:
        return np.ones(k)
    levels = np.array([10, -10, 5, -5, 0])
    if k % 512:
        return np.exp2(np.random.permutation(np.resize(levels, k // 32))).repeat(32)
    a = np.empty((k // 512, 16))
    for p in range(k // 512):
        a[p, :8] = np.random.permutation(np.resize(levels, 8))
        for g in range(8):
            far = levels[np.abs(levels - a[p, g]) >= 10]
            a[p, g + 8] = far[np.random.randint(len(far))]
    return np.exp2(a.ravel()).repeat(32)


def f64(x):
    return np.asarray(x).astype(np.float64)


def striped(idx):
    return np.tile(idx.reshape(-1, 16).T, (8, 1)).astype(np.uint16)


def unstriped(offs):
    return offs[:16].T.reshape(-1).astype(np.int64)


K, T, E, C, N = 1024, 512, 2, 256, 128


def by_expert(wq, xq):
    return np.concatenate([wq[e].T @ xq[:, e * C:(e + 1) * C] for e in range(E)], axis=1)


def setup_inputs():
    n = np.random.standard_normal
    s = mx_kscale(K)[:, None]
    return {
        "xT": (n((K, T)) * s).astype(np.float32),
        "w": (n((E, K, N)) / np.sqrt(K) / s[None]).astype(np.float32),
        "gate": np.tile(np.random.uniform(0.2, 1.0, E * C), (N, 1)).astype(np.float32),
        "offs": striped(np.random.permutation(T)[:E * C]),
    }


def reference(xT, w, gate, offs):
    idx = unstriped(offs)
    xq = mxq(f64(xT)[:, idx], 0, "e4m3")
    y = by_expert(mxq(f64(w), 1, "e4m3"), xq)
    out = np.zeros((N, T))
    out[:, idx] = f64(gate) * y
    return out

@@ -1,0 +1,165 @@
+from contextlib import ExitStack
+
+import concourse.mybir as mybir
+
+K, T, E, C, N = 1024, 512, 2, 256, 128
+FLOPS = 2 * K * N * E * C
+
+F32 = mybir.dt.float32
+BF16 = mybir.dt.bfloat16
+U32 = mybir.dt.uint32
+U16 = mybir.dt.uint16
+U8 = mybir.dt.uint8
+FP8X4 = mybir.dt.float8_e4m3fn_x4
+MULT = mybir.AluOpType.mult
+
+P = 128
+PACK = 4
+K_PASS = P * PACK
+PASSES = K // K_PASS
+LIST_COLS = C // 16
+
+
+def tile_routed_moe_kernel(tc, xT, w, gate, offs, out):
+    nc = tc.nc
+    with ExitStack() as ctx:
+        keep = ctx.enter_context(tc.tile_pool(name="keep", bufs=1))
+        psum = ctx.enter_context(tc.psum_pool(name="psum", bufs=1))
+
+        offsets = keep.tile([P, E * C // 16], U16, name="offsets")
+        nc.sync.dma_start(offsets[:], offs)
+
+        x_view = xT.rearrange("(g p t) n -> g p t n", p=P, t=PACK)
+        w_view = w.rearrange("e (g p j) n -> g p e (j n)", p=P, j=PACK)
+
+        planes = {}
+        w_raw = {}
+
+        def load_plane(g, t):
+            planes[(g, t)] = keep.tile([P, T], F32, name="plane%d%d" % (g, t))
+            nc.sync.dma_start(planes[(g, t)][:], x_view[g, :, t, :])
+
+        def load_w(g):
+            w_raw[g] = keep.tile([P, E, PACK * N], F32, name="w_raw%d" % g)
+            nc.sync.dma_start(w_raw[g][:], w_view[g])
+
+        load_plane(0, 0)
+        load_plane(0, 1)
+        load_w(0)
+        load_plane(0, 2)
+        load_plane(0, 3)
+        load_w(1)
+        for t in range(PACK):
+            load_plane(1, t)
+        gate_sb = keep.tile([P, E * C], F32, name="gate_sb")
+        nc.sync.dma_start(gate_sb[:], gate)
+
+        picked = {}
+        x_grouped = {}
+        x_codes = {}
+        x_scales = {}
+        w_grouped = {}
+        w_codes = {}
+        w_scales = {}
+        for g in range(PASSES):
+            for e in range(E):
+                picked[(g, e)] = keep.tile([P, PACK, C], F32, name="picked%d%d" % (g, e))
+                x_grouped[(g, e)] = keep.tile([P, C, PACK], BF16, name="x_grouped%d%d" % (g, e), align_bytes=64)
+                x_codes[(g, e)] = keep.tile([P, C], U32, name="x_codes%d%d" % (g, e), align_bytes=64)
+                x_scales[(g, e)] = keep.tile([P, C], U8, name="x_scales%d%d" % (g, e), align_bytes=64)
+            w_grouped[g] = keep.tile([P, E, N, PACK], BF16, name="w_grouped%d" % g, align_bytes=64)
+            w_codes[g] = keep.tile([P, E * N], U32, name="w_codes%d" % g, align_bytes=64)
+            w_scales[g] = keep.tile([P, E * N], U8, name="w_scales%d" % g, align_bytes=64)
+
+        def gather(g, t, e):
+            nc.vector.tensor_copy(
+                picked[(g, e)][:, t, :],
+                planes[(g, t)][:].indirect(offsets[:, e * LIST_COLS : (e + 1) * LIST_COLS]),
+            )
+
+        def group_x(g, e):
+            nc.scalar.copy(x_grouped[(g, e)][:], picked[(g, e)][:].rearrange("p t c -> p c t"))
+
+        def quantize_x(g, e):
+            nc.vector.quantize_mx(
+                out=x_codes[(g, e)][:].bitcast(FP8X4),
+                scales=x_scales[(g, e)][:],
+                in_=x_grouped[(g, e)][:].rearrange("p c t -> p (c t)"),
+            )
+
+        def group_w(g):
+            for e in range(E):
+                nc.scalar.copy(
+                    w_grouped[g][:, e, :, :],
+                    w_raw[g][:, e, :].rearrange("p (j n) -> p n j", j=PACK),
+                )
+
+        def quantize_w(g):
+            nc.vector.quantize_mx(
+                out=w_codes[g][:].bitcast(FP8X4),
+                scales=w_scales[g][:],
+                in_=w_grouped[g][:].rearrange("p e n j -> p (e n j)"),
+            )
+
+        sums = {}
+        for e in range(E):
+            sums[e] = psum.tile([P, C], F32, name="sums%d" % e)
+
+        def multiply(g, e):
+            cols = slice(e * N, (e + 1) * N)
+            nc.tensor.matmul_mx(
+                out=sums[e][:],
+                lhsT=w_codes[g][:, cols].bitcast(FP8X4),
+                lhsT_scale=w_scales[g][:, cols],
+                rhs=x_codes[(g, e)][:].bitcast(FP8X4),
+                rhs_scale=x_scales[(g, e)][:],
+                start=(g == 0),
+                stop=(g == PASSES - 1),
+            )
+
+        window = keep.tile([P, T], F32, name="window")
+        sums_sb = {}
+
+        def way_back(e):
+            sums_sb[e] = keep.tile([P, C], F32, name="sums_sb%d" % e)
+            nc.scalar.copy(sums_sb[e][:], sums[e][:])
+            nc.vector.tensor_tensor(
+                window[:].indirect(offsets[:, e * LIST_COLS : (e + 1) * LIST_COLS]),
+                sums_sb[e][:],
+                gate_sb[:, e * C : (e + 1) * C],
+                MULT,
+            )
+
+        for t in range(PACK):
+            for e in range(E):
+                gather(0, t, e)
+            if t == 1:
+                group_w(0)
+            if t == 2:
+                quantize_w(0)
+        group_x(0, 0)
+        group_x(0, 1)
+        group_w(1)
+        gather(1, 0, 0)
+        gather(1, 1, 0)
+        quantize_x(0, 0)
+        multiply(0, 0)
+        gather(1, 2, 0)
+        gather(1, 3, 0)
+        quantize_x(0, 1)
+        multiply(0, 1)
+        group_x(1, 0)
+        gather(1, 0, 1)
+        quantize_w(1)
+        gather(1, 1, 1)
+        gather(1, 2, 1)
+        quantize_x(1, 0)
+        multiply(1, 0)
+        gather(1, 3, 1)
+        group_x(1, 1)
+        way_back(0)
+        quantize_x(1, 1)
+        multiply(1, 1)
+        way_back(1)
+
+        nc.sync.dma_start(out, window[:])

@@ -12,6 +12,7 @@ U16 = mybir.dt.uint16
 U8 = mybir.dt.uint8
 FP8X4 = mybir.dt.float8_e4m3fn_x4
 MULT = mybir.AluOpType.mult
+COPY = mybir.ActivationFunctionType.Copy
 
 P = 128
 PACK = 4
@@ -32,12 +33,13 @@ def tile_routed_moe_kernel(tc, xT, w, gate, offs, out):
         x_view = xT.rearrange("(g p t) n -> g p t n", p=P, t=PACK)
         w_view = w.rearrange("e (g p j) n -> g p e (j n)", p=P, j=PACK)
 
-        planes = {}
+        raw = {}
         w_raw = {}
+        for g in range(PASSES):
+            raw[g] = keep.tile([P, PACK, T], F32, name="raw%d" % g)
 
         def load_plane(g, t):
-            planes[(g, t)] = keep.tile([P, T], F32, name="plane%d%d" % (g, t))
-            nc.sync.dma_start(planes[(g, t)][:], x_view[g, :, t, :])
+            nc.sync.dma_start(raw[g][:, t, :], x_view[g, :, t, :])
 
         def load_w(g):
             w_raw[g] = keep.tile([P, E, PACK * N], F32, name="w_raw%d" % g)
@@ -54,7 +56,6 @@ def tile_routed_moe_kernel(tc, xT, w, gate, offs, out):
         gate_sb = keep.tile([P, E * C], F32, name="gate_sb")
         nc.sync.dma_start(gate_sb[:], gate)
 
-        picked = {}
         x_grouped = {}
         x_codes = {}
         x_scales = {}
@@ -63,7 +64,6 @@ def tile_routed_moe_kernel(tc, xT, w, gate, offs, out):
         w_scales = {}
         for g in range(PASSES):
             for e in range(E):
-                picked[(g, e)] = keep.tile([P, PACK, C], F32, name="picked%d%d" % (g, e))
                 x_grouped[(g, e)] = keep.tile([P, C, PACK], BF16, name="x_grouped%d%d" % (g, e), align_bytes=64)
                 x_codes[(g, e)] = keep.tile([P, C], U32, name="x_codes%d%d" % (g, e), align_bytes=64)
                 x_scales[(g, e)] = keep.tile([P, C], U8, name="x_scales%d%d" % (g, e), align_bytes=64)
@@ -73,12 +73,9 @@ def tile_routed_moe_kernel(tc, xT, w, gate, offs, out):
 
         def gather(g, t, e):
             nc.vector.tensor_copy(
-                picked[(g, e)][:, t, :],
-                planes[(g, t)][:].indirect(offsets[:, e * LIST_COLS : (e + 1) * LIST_COLS]),
+                x_grouped[(g, e)][:, :, t],
+                raw[g][:, t, :].indirect(offsets[:, e * LIST_COLS : (e + 1) * LIST_COLS]),
             )
-
-        def group_x(g, e):
-            nc.scalar.copy(x_grouped[(g, e)][:], picked[(g, e)][:].rearrange("p t c -> p c t"))
 
         def quantize_x(g, e):
             nc.vector.quantize_mx(
@@ -120,9 +117,11 @@ def tile_routed_moe_kernel(tc, xT, w, gate, offs, out):
         window = keep.tile([P, T], F32, name="window")
         sums_sb = {}
 
-        def way_back(e):
+        def empty_bank(e):
             sums_sb[e] = keep.tile([P, C], F32, name="sums_sb%d" % e)
             nc.scalar.copy(sums_sb[e][:], sums[e][:])
+
+        def scatter(e):
             nc.vector.tensor_tensor(
                 window[:].indirect(offsets[:, e * LIST_COLS : (e + 1) * LIST_COLS]),
                 sums_sb[e][:],
@@ -130,36 +129,33 @@ def tile_routed_moe_kernel(tc, xT, w, gate, offs, out):
                 MULT,
             )
 
+        group_w(0)
         for t in range(PACK):
             for e in range(E):
                 gather(0, t, e)
-            if t == 1:
-                group_w(0)
             if t == 2:
                 quantize_w(0)
-        group_x(0, 0)
-        group_x(0, 1)
         group_w(1)
         gather(1, 0, 0)
-        gather(1, 1, 0)
         quantize_x(0, 0)
         multiply(0, 0)
-        gather(1, 2, 0)
-        gather(1, 3, 0)
+        gather(1, 1, 0)
         quantize_x(0, 1)
         multiply(0, 1)
-        group_x(1, 0)
-        gather(1, 0, 1)
+        gather(1, 2, 0)
         quantize_w(1)
-        gather(1, 1, 1)
-        gather(1, 2, 1)
+        gather(1, 3, 0)
+        gather(1, 0, 1)
         quantize_x(1, 0)
         multiply(1, 0)
+        empty_bank(0)
+        gather(1, 1, 1)
+        gather(1, 2, 1)
         gather(1, 3, 1)
-        group_x(1, 1)
-        way_back(0)
         quantize_x(1, 1)
         multiply(1, 1)
-        way_back(1)
+        empty_bank(1)
+        scatter(0)
+        scatter(1)
 
         nc.sync.dma_start(out, window[:])

@@ -21,6 +21,10 @@ PASSES = K // K_PASS
 LIST_COLS = C // 16
 
 
+W_ENGINE = "gpsimd"
+IL01_ENGINE = "gpsimd"
+
+
 def tile_routed_moe_kernel(tc, xT, w, gate, offs, out):
     nc = tc.nc
     with ExitStack() as ctx:
@@ -33,13 +37,12 @@ def tile_routed_moe_kernel(tc, xT, w, gate, offs, out):
         x_view = xT.rearrange("(g p t) n -> g p t n", p=P, t=PACK)
         w_view = w.rearrange("e (g p j) n -> g p e (j n)", p=P, j=PACK)
 
-        raw = {}
+        planes = {}
         w_raw = {}
-        for g in range(PASSES):
-            raw[g] = keep.tile([P, PACK, T], F32, name="raw%d" % g)
 
         def load_plane(g, t):
-            nc.sync.dma_start(raw[g][:, t, :], x_view[g, :, t, :])
+            planes[(g, t)] = keep.tile([P, T], F32, name="plane%d%d" % (g, t))
+            nc.sync.dma_start(planes[(g, t)][:], x_view[g, :, t, :])
 
         def load_w(g):
             w_raw[g] = keep.tile([P, E, PACK * N], F32, name="w_raw%d" % g)
@@ -47,15 +50,18 @@ def tile_routed_moe_kernel(tc, xT, w, gate, offs, out):
 
         load_plane(0, 0)
         load_plane(0, 1)
+        pair_f32 = keep.tile([P, 2, T], F32, name="pair_f32")
+        nc.sync.dma_start(pair_f32[:], x_view[0, :, 2:4, :])
+        load_plane(1, 0)
+        load_plane(1, 1)
         load_w(0)
-        load_plane(0, 2)
-        load_plane(0, 3)
+        load_plane(1, 2)
+        load_plane(1, 3)
         load_w(1)
-        for t in range(PACK):
-            load_plane(1, t)
         gate_sb = keep.tile([P, E * C], F32, name="gate_sb")
         nc.sync.dma_start(gate_sb[:], gate)
 
+        picked = {}
         x_grouped = {}
         x_codes = {}
         x_scales = {}
@@ -64,18 +70,37 @@ def tile_routed_moe_kernel(tc, xT, w, gate, offs, out):
         w_scales = {}
         for g in range(PASSES):
             for e in range(E):
+                picked[(g, e)] = keep.tile([P, 2 if g == 0 else PACK, C], F32, name="picked%d%d" % (g, e))
                 x_grouped[(g, e)] = keep.tile([P, C, PACK], BF16, name="x_grouped%d%d" % (g, e), align_bytes=64)
                 x_codes[(g, e)] = keep.tile([P, C], U32, name="x_codes%d%d" % (g, e), align_bytes=64)
                 x_scales[(g, e)] = keep.tile([P, C], U8, name="x_scales%d%d" % (g, e), align_bytes=64)
             w_grouped[g] = keep.tile([P, E, N, PACK], BF16, name="w_grouped%d" % g, align_bytes=64)
             w_codes[g] = keep.tile([P, E * N], U32, name="w_codes%d" % g, align_bytes=64)
             w_scales[g] = keep.tile([P, E * N], U8, name="w_scales%d" % g, align_bytes=64)
+        pair_bf16 = keep.tile([P, 2, T], BF16, name="pair_bf16")
+
+        def slots(e):
+            return offsets[:, e * LIST_COLS : (e + 1) * LIST_COLS]
+
+        def plain_copy(engine, dst, src):
+            if engine == "scalar":
+                nc.scalar.copy(dst, src)
+            elif engine == "gpsimd":
+                nc.gpsimd.tensor_copy(dst, src)
+            else:
+                nc.vector.tensor_copy(dst, src)
 
         def gather(g, t, e):
-            nc.vector.tensor_copy(
-                x_grouped[(g, e)][:, :, t],
-                raw[g][:, t, :].indirect(offsets[:, e * LIST_COLS : (e + 1) * LIST_COLS]),
-            )
+            nc.vector.tensor_copy(picked[(g, e)][:, t, :], planes[(g, t)][:].indirect(slots(e)))
+
+        def gather_scalar(i, e):
+            nc.scalar.activation(x_grouped[(0, e)][:, :, 2 + i], pair_bf16[:, i, :].indirect(slots(e)), COPY)
+
+        def group_x01(e):
+            plain_copy(IL01_ENGINE, x_grouped[(0, e)][:, :, 0:2], picked[(0, e)][:].rearrange("p t c -> p c t"))
+
+        def group_x(g, e):
+            nc.scalar.copy(x_grouped[(g, e)][:], picked[(g, e)][:].rearrange("p t c -> p c t"))
 
         def quantize_x(g, e):
             nc.vector.quantize_mx(
@@ -86,7 +111,8 @@ def tile_routed_moe_kernel(tc, xT, w, gate, offs, out):
 
         def group_w(g):
             for e in range(E):
-                nc.scalar.copy(
+                plain_copy(
+                    W_ENGINE,
                     w_grouped[g][:, e, :, :],
                     w_raw[g][:, e, :].rearrange("p (j n) -> p n j", j=PACK),
                 )
@@ -117,44 +143,47 @@ def tile_routed_moe_kernel(tc, xT, w, gate, offs, out):
         window = keep.tile([P, T], F32, name="window")
         sums_sb = {}
 
-        def empty_bank(e):
+        def empty_bank(engine, e):
             sums_sb[e] = keep.tile([P, C], F32, name="sums_sb%d" % e)
-            nc.scalar.copy(sums_sb[e][:], sums[e][:])
+            plain_copy(engine, sums_sb[e][:], sums[e][:])
 
         def scatter(e):
-            nc.vector.tensor_tensor(
-                window[:].indirect(offsets[:, e * LIST_COLS : (e + 1) * LIST_COLS]),
-                sums_sb[e][:],
-                gate_sb[:, e * C : (e + 1) * C],
-                MULT,
-            )
+            nc.vector.tensor_tensor(window[:].indirect(slots(e)), sums_sb[e][:], gate_sb[:, e * C : (e + 1) * C], MULT)
 
-        group_w(0)
-        for t in range(PACK):
-            for e in range(E):
-                gather(0, t, e)
-            if t == 2:
-                quantize_w(0)
-        group_w(1)
+        gather(0, 0, 0)
+        gather(0, 0, 1)
+        gather(0, 1, 0)
+        gather(0, 1, 1)
+        nc.scalar.copy(pair_bf16[:], pair_f32[:])
+        group_x01(0)
+        group_x01(1)
+        for e in range(E):
+            gather_scalar(0, e)
+            gather_scalar(1, e)
         gather(1, 0, 0)
-        quantize_x(0, 0)
-        multiply(0, 0)
-        gather(1, 1, 0)
-        quantize_x(0, 1)
-        multiply(0, 1)
-        gather(1, 2, 0)
-        quantize_w(1)
-        gather(1, 3, 0)
         gather(1, 0, 1)
-        quantize_x(1, 0)
-        multiply(1, 0)
-        empty_bank(0)
+        gather(1, 1, 0)
         gather(1, 1, 1)
+        group_w(0)
+        gather(1, 2, 0)
+        gather(1, 3, 0)
+        group_x(1, 0)
         gather(1, 2, 1)
         gather(1, 3, 1)
+        group_w(1)
+        group_x(1, 1)
+        quantize_w(0)
+        quantize_x(0, 0)
+        multiply(0, 0)
+        quantize_x(0, 1)
+        multiply(0, 1)
+        quantize_w(1)
+        quantize_x(1, 0)
+        multiply(1, 0)
+        empty_bank("vector", 0)
         quantize_x(1, 1)
         multiply(1, 1)
-        empty_bank(1)
+        empty_bank("scalar", 1)
         scatter(0)
         scatter(1)
 

@@ -21,10 +21,6 @@ PASSES = K // K_PASS
 LIST_COLS = C // 16
 
 
-W_ENGINE = "gpsimd"
-IL01_ENGINE = "gpsimd"
-
-
 def tile_routed_moe_kernel(tc, xT, w, gate, offs, out):
     nc = tc.nc
     with ExitStack() as ctx:
@@ -40,13 +36,13 @@ def tile_routed_moe_kernel(tc, xT, w, gate, offs, out):
         planes = {}
         w_raw = {}
 
-        def load_plane(g, t):
-            planes[(g, t)] = keep.tile([P, T], F32, name="plane%d%d" % (g, t))
+        def load_plane(g, t, link=""):
+            planes[(g, t)] = keep.tile([P, T], F32, name="plane%d%d" % (g, t), tag=link or "plane%d%d" % (g, t), align_bytes=64)
             nc.sync.dma_start(planes[(g, t)][:], x_view[g, :, t, :])
 
-        def load_w(g):
-            w_raw[g] = keep.tile([P, E, PACK * N], F32, name="w_raw%d" % g)
-            nc.sync.dma_start(w_raw[g][:], w_view[g])
+        def load_w(g, e):
+            w_raw[(g, e)] = keep.tile([P, PACK * N], F32, name="w_raw%d%d" % (g, e))
+            nc.sync.dma_start(w_raw[(g, e)][:], w_view[g, :, e, :])
 
         load_plane(0, 0)
         load_plane(0, 1)
@@ -54,41 +50,39 @@ def tile_routed_moe_kernel(tc, xT, w, gate, offs, out):
         nc.sync.dma_start(pair_f32[:], x_view[0, :, 2:4, :])
         load_plane(1, 0)
         load_plane(1, 1)
-        load_w(0)
+        load_w(0, 0)
+        load_w(0, 1)
         load_plane(1, 2)
-        load_plane(1, 3)
-        load_w(1)
+        load_w(1, 0)
+        load_plane(1, 3, "link0")
+        load_w(1, 1)
         gate_sb = keep.tile([P, E * C], F32, name="gate_sb")
         nc.sync.dma_start(gate_sb[:], gate)
 
-        picked = {}
-        x_grouped = {}
+        picked = {
+            (0, 0): keep.tile([P, 2, C], F32, name="picked00"),
+            (0, 1): keep.tile([P, 2, C], F32, name="picked01"),
+            (1, 0): keep.tile([P, PACK, C], F32, name="picked10", tag="link1", align_bytes=64),
+            (1, 1): keep.tile([P, PACK, C], F32, name="picked11"),
+        }
+        w_grouped = {
+            0: keep.tile([P, E, N, PACK], BF16, name="w_grouped0", tag="link2", align_bytes=64),
+            1: keep.tile([P, E, N, PACK], BF16, name="w_grouped1", align_bytes=64),
+        }
+        x_grouped = {
+            (0, 0): keep.tile([P, C, PACK], BF16, name="x_grouped00", align_bytes=64),
+            (1, 0): keep.tile([P, C, PACK], BF16, name="x_grouped10", align_bytes=64),
+            (0, 1): keep.tile([P, C, PACK], BF16, name="x_grouped01", align_bytes=64),
+            (1, 1): keep.tile([P, C, PACK], BF16, name="x_grouped11", align_bytes=64),
+        }
+        pair_bf16 = keep.tile([P, 2, T], BF16, name="pair_bf16")
         x_codes = {}
         x_scales = {}
-        w_grouped = {}
         w_codes = {}
         w_scales = {}
-        for g in range(PASSES):
-            for e in range(E):
-                picked[(g, e)] = keep.tile([P, 2 if g == 0 else PACK, C], F32, name="picked%d%d" % (g, e))
-                x_grouped[(g, e)] = keep.tile([P, C, PACK], BF16, name="x_grouped%d%d" % (g, e), align_bytes=64)
-                x_codes[(g, e)] = keep.tile([P, C], U32, name="x_codes%d%d" % (g, e), align_bytes=64)
-                x_scales[(g, e)] = keep.tile([P, C], U8, name="x_scales%d%d" % (g, e), align_bytes=64)
-            w_grouped[g] = keep.tile([P, E, N, PACK], BF16, name="w_grouped%d" % g, align_bytes=64)
-            w_codes[g] = keep.tile([P, E * N], U32, name="w_codes%d" % g, align_bytes=64)
-            w_scales[g] = keep.tile([P, E * N], U8, name="w_scales%d" % g, align_bytes=64)
-        pair_bf16 = keep.tile([P, 2, T], BF16, name="pair_bf16")
 
         def slots(e):
             return offsets[:, e * LIST_COLS : (e + 1) * LIST_COLS]
-
-        def plain_copy(engine, dst, src):
-            if engine == "scalar":
-                nc.scalar.copy(dst, src)
-            elif engine == "gpsimd":
-                nc.gpsimd.tensor_copy(dst, src)
-            else:
-                nc.vector.tensor_copy(dst, src)
 
         def gather(g, t, e):
             nc.vector.tensor_copy(picked[(g, e)][:, t, :], planes[(g, t)][:].indirect(slots(e)))
@@ -97,12 +91,11 @@ def tile_routed_moe_kernel(tc, xT, w, gate, offs, out):
             nc.scalar.activation(x_grouped[(0, e)][:, :, 2 + i], pair_bf16[:, i, :].indirect(slots(e)), COPY)
 
         def group_x01(e):
-            plain_copy(IL01_ENGINE, x_grouped[(0, e)][:, :, 0:2], picked[(0, e)][:].rearrange("p t c -> p c t"))
+            nc.gpsimd.tensor_copy(x_grouped[(0, e)][:, :, 0:2], picked[(0, e)][:].rearrange("p t c -> p c t"))
 
-        def group_x(g, e):
-            nc.scalar.copy(x_grouped[(g, e)][:], picked[(g, e)][:].rearrange("p t c -> p c t"))
-
-        def quantize_x(g, e):
+        def quantize_x(g, e, link):
+            x_codes[(g, e)] = keep.tile([P, C], U32, name="x_codes%d%d" % (g, e), tag=link or "x_codes%d%d" % (g, e), align_bytes=64)
+            x_scales[(g, e)] = keep.tile([P, C], U8, name="x_scales%d%d" % (g, e), align_bytes=64)
             nc.vector.quantize_mx(
                 out=x_codes[(g, e)][:].bitcast(FP8X4),
                 scales=x_scales[(g, e)][:],
@@ -111,13 +104,14 @@ def tile_routed_moe_kernel(tc, xT, w, gate, offs, out):
 
         def group_w(g):
             for e in range(E):
-                plain_copy(
-                    W_ENGINE,
+                nc.gpsimd.tensor_copy(
                     w_grouped[g][:, e, :, :],
-                    w_raw[g][:, e, :].rearrange("p (j n) -> p n j", j=PACK),
+                    w_raw[(g, e)][:].rearrange("p (j n) -> p n j", j=PACK),
                 )
 
-        def quantize_w(g):
+        def quantize_w(g, link):
+            w_codes[g] = keep.tile([P, E * N], U32, name="w_codes%d" % g, tag=link or "w_codes%d" % g, align_bytes=64)
+            w_scales[g] = keep.tile([P, E * N], U8, name="w_scales%d" % g, align_bytes=64)
             nc.vector.quantize_mx(
                 out=w_codes[g][:].bitcast(FP8X4),
                 scales=w_scales[g][:],
@@ -143,9 +137,12 @@ def tile_routed_moe_kernel(tc, xT, w, gate, offs, out):
         window = keep.tile([P, T], F32, name="window")
         sums_sb = {}
 
-        def empty_bank(engine, e):
+        def empty_bank(e):
             sums_sb[e] = keep.tile([P, C], F32, name="sums_sb%d" % e)
-            plain_copy(engine, sums_sb[e][:], sums[e][:])
+            if e == 0:
+                nc.vector.tensor_copy(sums_sb[e][:], sums[e][:])
+            else:
+                nc.scalar.copy(sums_sb[e][:], sums[e][:])
 
         def scatter(e):
             nc.vector.tensor_tensor(window[:].indirect(slots(e)), sums_sb[e][:], gate_sb[:, e * C : (e + 1) * C], MULT)
@@ -160,30 +157,26 @@ def tile_routed_moe_kernel(tc, xT, w, gate, offs, out):
         for e in range(E):
             gather_scalar(0, e)
             gather_scalar(1, e)
-        gather(1, 0, 0)
-        gather(1, 0, 1)
-        gather(1, 1, 0)
-        gather(1, 1, 1)
-        group_w(0)
-        gather(1, 2, 0)
-        gather(1, 3, 0)
-        group_x(1, 0)
-        gather(1, 2, 1)
-        gather(1, 3, 1)
+        for t in range(PACK):
+            gather(1, t, 0)
+            gather(1, t, 1)
+            if t == 1:
+                group_w(0)
         group_w(1)
-        group_x(1, 1)
-        quantize_w(0)
-        quantize_x(0, 0)
+        nc.vector.tensor_copy(x_grouped[(1, 0)][:], picked[(1, 0)][:].rearrange("p t c -> p c t"))
+        nc.scalar.copy(x_grouped[(1, 1)][:], picked[(1, 1)][:].rearrange("p t c -> p c t"))
+        quantize_w(0, "link0")
+        quantize_w(1, "")
+        quantize_x(0, 0, "link1")
         multiply(0, 0)
-        quantize_x(0, 1)
-        multiply(0, 1)
-        quantize_w(1)
-        quantize_x(1, 0)
+        quantize_x(1, 0, "")
         multiply(1, 0)
-        empty_bank("vector", 0)
-        quantize_x(1, 1)
+        empty_bank(0)
+        quantize_x(0, 1, "link2")
+        multiply(0, 1)
+        quantize_x(1, 1, "")
         multiply(1, 1)
-        empty_bank("scalar", 1)
+        empty_bank(1)
         scatter(0)
         scatter(1)
 

@@ -18,7 +18,10 @@ P = 128
 PACK = 4
 K_PASS = P * PACK
 PASSES = K // K_PASS
+S = E * C
 LIST_COLS = C // 16
+SCALAR_PASS = 0
+VECTOR_PASS = 1
 
 
 def tile_routed_moe_kernel(tc, xT, w, gate, offs, out):
@@ -27,55 +30,53 @@ def tile_routed_moe_kernel(tc, xT, w, gate, offs, out):
         keep = ctx.enter_context(tc.tile_pool(name="keep", bufs=1))
         psum = ctx.enter_context(tc.psum_pool(name="psum", bufs=1))
 
-        offsets = keep.tile([P, E * C // 16], U16, name="offsets")
+        offsets = keep.tile([P, S // 16], U16, name="offsets")
         nc.sync.dma_start(offsets[:], offs)
 
         x_view = xT.rearrange("(g p t) n -> g p t n", p=P, t=PACK)
         w_view = w.rearrange("e (g p j) n -> g p e (j n)", p=P, j=PACK)
 
-        planes = {}
+        v_raw = keep.tile([P, PACK * T], F32, name="v_raw")
+        s_raw = {}
         w_raw = {}
 
-        def load_plane(g, t, link=""):
-            planes[(g, t)] = keep.tile([P, T], F32, name="plane%d%d" % (g, t), tag=link or "plane%d%d" % (g, t), align_bytes=64)
-            nc.sync.dma_start(planes[(g, t)][:], x_view[g, :, t, :])
+        def v_cols(t, planes=1):
+            return slice((PACK - 1 - t) * T, (PACK - 1 - t + planes) * T)
+
+        def load_v(t):
+            nc.sync.dma_start(v_raw[:, v_cols(t)], x_view[VECTOR_PASS, :, t, :])
+
+        def load_s(t):
+            s_raw[t] = keep.tile([P, T], F32, name="s_raw%d" % t, tag="link" if t == PACK - 1 else "s_raw%d" % t, align_bytes=64)
+            nc.sync.dma_start(s_raw[t][:], x_view[SCALAR_PASS, :, t, :])
 
         def load_w(g, e):
             w_raw[(g, e)] = keep.tile([P, PACK * N], F32, name="w_raw%d%d" % (g, e))
             nc.sync.dma_start(w_raw[(g, e)][:], w_view[g, :, e, :])
 
-        load_plane(0, 0)
-        load_plane(0, 1)
-        pair_f32 = keep.tile([P, 2, T], F32, name="pair_f32")
-        nc.sync.dma_start(pair_f32[:], x_view[0, :, 2:4, :])
-        load_plane(1, 0)
-        load_plane(1, 1)
-        load_w(0, 0)
-        load_w(0, 1)
-        load_plane(1, 2)
-        load_w(1, 0)
-        load_plane(1, 3, "link0")
-        load_w(1, 1)
-        gate_sb = keep.tile([P, E * C], F32, name="gate_sb")
+        load_v(0)
+        load_s(0)
+        load_s(1)
+        load_v(1)
+        load_s(2)
+        load_v(2)
+        load_s(3)
+        load_v(3)
+        for e in range(E):
+            for g in range(PASSES):
+                load_w(g, e)
+        gate_sb = keep.tile([P, S], F32, name="gate_sb")
         nc.sync.dma_start(gate_sb[:], gate)
 
-        picked = {
-            (0, 0): keep.tile([P, 2, C], F32, name="picked00"),
-            (0, 1): keep.tile([P, 2, C], F32, name="picked01"),
-            (1, 0): keep.tile([P, PACK, C], F32, name="picked10", tag="link1", align_bytes=64),
-            (1, 1): keep.tile([P, PACK, C], F32, name="picked11"),
-        }
-        w_grouped = {
-            0: keep.tile([P, E, N, PACK], BF16, name="w_grouped0", tag="link2", align_bytes=64),
-            1: keep.tile([P, E, N, PACK], BF16, name="w_grouped1", align_bytes=64),
-        }
-        x_grouped = {
-            (0, 0): keep.tile([P, C, PACK], BF16, name="x_grouped00", align_bytes=64),
-            (1, 0): keep.tile([P, C, PACK], BF16, name="x_grouped10", align_bytes=64),
-            (0, 1): keep.tile([P, C, PACK], BF16, name="x_grouped01", align_bytes=64),
-            (1, 1): keep.tile([P, C, PACK], BF16, name="x_grouped11", align_bytes=64),
-        }
-        pair_bf16 = keep.tile([P, 2, T], BF16, name="pair_bf16")
+        s_bf16 = keep.tile([P, PACK, T], BF16, name="s_bf16")
+        picked = keep.tile([P, PACK, S], F32, name="picked")
+        x_grouped = {}
+        w_grouped = {}
+        for e in range(E):
+            w_grouped[e] = keep.tile([P, PASSES, N, PACK], BF16, name="w_grouped%d" % e, align_bytes=64)
+            for g in range(PASSES):
+                if (g, e) != (SCALAR_PASS, 1):
+                    x_grouped[(g, e)] = keep.tile([P, C, PACK], BF16, name="x_grouped%d%d" % (g, e), align_bytes=64)
         x_codes = {}
         x_scales = {}
         w_codes = {}
@@ -84,17 +85,26 @@ def tile_routed_moe_kernel(tc, xT, w, gate, offs, out):
         def slots(e):
             return offsets[:, e * LIST_COLS : (e + 1) * LIST_COLS]
 
-        def gather(g, t, e):
-            nc.vector.tensor_copy(picked[(g, e)][:, t, :], planes[(g, t)][:].indirect(slots(e)))
+        def of_expert(e):
+            return slice(e * C, (e + 1) * C)
 
-        def gather_scalar(i, e):
-            nc.scalar.activation(x_grouped[(0, e)][:, :, 2 + i], pair_bf16[:, i, :].indirect(slots(e)), COPY)
+        def gather_half(t, e):
+            nc.vector.tensor_copy(picked[:, t, of_expert(e)], v_raw[:, v_cols(t)].indirect(slots(e)))
 
-        def group_x01(e):
-            nc.gpsimd.tensor_copy(x_grouped[(0, e)][:, :, 0:2], picked[(0, e)][:].rearrange("p t c -> p c t"))
+        def gather_all(t):
+            nc.vector.tensor_copy(picked[:, t, :], v_raw[:, v_cols(t, 2)].indirect(offsets[:]))
 
-        def quantize_x(g, e, link):
-            x_codes[(g, e)] = keep.tile([P, C], U32, name="x_codes%d%d" % (g, e), tag=link or "x_codes%d%d" % (g, e), align_bytes=64)
+        def cast_plane(t):
+            nc.gpsimd.tensor_copy(s_bf16[:, t, :], s_raw[t][:])
+
+        def gather_scalar(t, e):
+            nc.scalar.activation(x_grouped[(SCALAR_PASS, e)][:, :, t], s_bf16[:, t, :].indirect(slots(e)), COPY)
+
+        def group_x(e):
+            nc.vector.tensor_copy(x_grouped[(VECTOR_PASS, e)][:], picked[:, :, of_expert(e)].rearrange("p t c -> p c t"))
+
+        def quantize_x(g, e):
+            x_codes[(g, e)] = keep.tile([P, C], U32, name="x_codes%d%d" % (g, e), align_bytes=64)
             x_scales[(g, e)] = keep.tile([P, C], U8, name="x_scales%d%d" % (g, e), align_bytes=64)
             nc.vector.quantize_mx(
                 out=x_codes[(g, e)][:].bitcast(FP8X4),
@@ -102,82 +112,93 @@ def tile_routed_moe_kernel(tc, xT, w, gate, offs, out):
                 in_=x_grouped[(g, e)][:].rearrange("p c t -> p (c t)"),
             )
 
-        def group_w(g):
-            for e in range(E):
-                nc.gpsimd.tensor_copy(
-                    w_grouped[g][:, e, :, :],
-                    w_raw[(g, e)][:].rearrange("p (j n) -> p n j", j=PACK),
-                )
+        def group_w(g, e):
+            nc.vector.tensor_copy(
+                w_grouped[e][:, g, :, :],
+                w_raw[(g, e)][:].rearrange("p (j n) -> p n j", j=PACK),
+            )
 
-        def quantize_w(g, link):
-            w_codes[g] = keep.tile([P, E * N], U32, name="w_codes%d" % g, tag=link or "w_codes%d" % g, align_bytes=64)
-            w_scales[g] = keep.tile([P, E * N], U8, name="w_scales%d" % g, align_bytes=64)
+        def quantize_w(e):
+            w_codes[e] = keep.tile([P, PASSES * N], U32, name="w_codes%d" % e, align_bytes=64)
+            w_scales[e] = keep.tile([P, PASSES * N], U8, name="w_scales%d" % e, align_bytes=64)
             nc.vector.quantize_mx(
-                out=w_codes[g][:].bitcast(FP8X4),
-                scales=w_scales[g][:],
-                in_=w_grouped[g][:].rearrange("p e n j -> p (e n j)"),
+                out=w_codes[e][:].bitcast(FP8X4),
+                scales=w_scales[e][:],
+                in_=w_grouped[e][:].rearrange("p g n j -> p (g n j)"),
             )
 
         sums = {}
         for e in range(E):
             sums[e] = psum.tile([P, C], F32, name="sums%d" % e)
 
-        def multiply(g, e):
-            cols = slice(e * N, (e + 1) * N)
+        def multiply(g, e, first):
+            w_cols = slice(g * N, (g + 1) * N)
             nc.tensor.matmul_mx(
                 out=sums[e][:],
-                lhsT=w_codes[g][:, cols].bitcast(FP8X4),
-                lhsT_scale=w_scales[g][:, cols],
+                lhsT=w_codes[e][:, w_cols].bitcast(FP8X4),
+                lhsT_scale=w_scales[e][:, w_cols],
                 rhs=x_codes[(g, e)][:].bitcast(FP8X4),
                 rhs_scale=x_scales[(g, e)][:],
-                start=(g == 0),
-                stop=(g == PASSES - 1),
+                start=first,
+                stop=not first,
             )
 
         window = keep.tile([P, T], F32, name="window")
         sums_sb = {}
 
+        HALF = C // 2
+
+        def empty_half(e, h):
+            sums_sb[(e, h)] = keep.tile([P, HALF], F32, name="sums_sb%d%d" % (e, h))
+            if h == 0:
+                nc.vector.tensor_copy(sums_sb[(e, h)][:], sums[e][:, 0:HALF])
+            else:
+                nc.scalar.copy(sums_sb[(e, h)][:], sums[e][:, HALF:C])
+
+        def scatter_half(e, h):
+            first = e * C + h * HALF
+            nc.vector.tensor_tensor(
+                window[:].indirect(offsets[:, first // 16 : (first + HALF) // 16]),
+                sums_sb[(e, h)][:],
+                gate_sb[:, first : first + HALF],
+                MULT,
+            )
+
         def empty_bank(e):
             sums_sb[e] = keep.tile([P, C], F32, name="sums_sb%d" % e)
-            if e == 0:
-                nc.vector.tensor_copy(sums_sb[e][:], sums[e][:])
-            else:
-                nc.scalar.copy(sums_sb[e][:], sums[e][:])
+            nc.scalar.copy(sums_sb[e][:], sums[e][:])
 
         def scatter(e):
-            nc.vector.tensor_tensor(window[:].indirect(slots(e)), sums_sb[e][:], gate_sb[:, e * C : (e + 1) * C], MULT)
+            nc.vector.tensor_tensor(window[:].indirect(slots(e)), sums_sb[e][:], gate_sb[:, of_expert(e)], MULT)
 
-        gather(0, 0, 0)
-        gather(0, 0, 1)
-        gather(0, 1, 0)
-        gather(0, 1, 1)
-        nc.scalar.copy(pair_bf16[:], pair_f32[:])
-        group_x01(0)
-        group_x01(1)
-        for e in range(E):
-            gather_scalar(0, e)
-            gather_scalar(1, e)
+        gather_half(0, 0)
+        gather_half(0, 1)
         for t in range(PACK):
-            gather(1, t, 0)
-            gather(1, t, 1)
-            if t == 1:
-                group_w(0)
-        group_w(1)
-        nc.vector.tensor_copy(x_grouped[(1, 0)][:], picked[(1, 0)][:].rearrange("p t c -> p c t"))
-        nc.scalar.copy(x_grouped[(1, 1)][:], picked[(1, 1)][:].rearrange("p t c -> p c t"))
-        quantize_w(0, "link0")
-        quantize_w(1, "")
-        quantize_x(0, 0, "link1")
-        multiply(0, 0)
-        quantize_x(1, 0, "")
-        multiply(1, 0)
-        empty_bank(0)
-        quantize_x(0, 1, "link2")
-        multiply(0, 1)
-        quantize_x(1, 1, "")
-        multiply(1, 1)
-        empty_bank(1)
-        scatter(0)
+            cast_plane(t)
+            gather_scalar(t, 0)
+            if t > 0:
+                gather_all(t)
+        x_grouped[(SCALAR_PASS, 1)] = keep.tile([P, C, PACK], BF16, name="x_grouped_late", tag="link", align_bytes=64)
+        for t in range(PACK):
+            gather_scalar(t, 1)
+        for e in range(E):
+            for g in range(PASSES):
+                group_w(g, e)
+        for e in range(E):
+            group_x(e)
+        for e in range(E):
+            quantize_w(e)
+            quantize_x(VECTOR_PASS, e)
+            multiply(VECTOR_PASS, e, True)
+            quantize_x(SCALAR_PASS, e)
+            multiply(SCALAR_PASS, e, False)
+            if e == 0:
+                empty_half(0, 0)
+                empty_half(0, 1)
+            else:
+                empty_bank(1)
+        scatter_half(0, 0)
+        scatter_half(0, 1)
         scatter(1)
 
         nc.sync.dma_start(out, window[:])

@@ -101,7 +101,10 @@ def tile_routed_moe_kernel(tc, xT, w, gate, offs, out):
             nc.scalar.activation(x_grouped[(SCALAR_PASS, e)][:, :, t], s_bf16[:, t, :].indirect(slots(e)), COPY)
 
         def group_x(e):
-            nc.vector.tensor_copy(x_grouped[(VECTOR_PASS, e)][:], picked[:, :, of_expert(e)].rearrange("p t c -> p c t"))
+            nc.vector.tensor_copy(
+                x_grouped[(VECTOR_PASS, e)][:].rearrange("p (c i) t -> p c t i", i=4),
+                picked[:, :, of_expert(e)].rearrange("p t (c i) -> p c t i", i=4),
+            )
 
         def quantize_x(g, e):
             x_codes[(g, e)] = keep.tile([P, C], U32, name="x_codes%d%d" % (g, e), align_bytes=64)
@@ -114,8 +117,8 @@ def tile_routed_moe_kernel(tc, xT, w, gate, offs, out):
 
         def group_w(g, e):
             nc.vector.tensor_copy(
-                w_grouped[e][:, g, :, :],
-                w_raw[(g, e)][:].rearrange("p (j n) -> p n j", j=PACK),
+                w_grouped[e][:, g, :, :].rearrange("p (c i) j -> p c j i", i=4),
+                w_raw[(g, e)][:].rearrange("p (j c i) -> p c j i", j=PACK, i=4),
             )
 
         def quantize_w(e):

@@ -54,14 +54,9 @@ def tile_routed_moe_kernel(tc, xT, w, gate, offs, out):
             w_raw[(g, e)] = keep.tile([P, PACK * N], F32, name="w_raw%d%d" % (g, e))
             nc.sync.dma_start(w_raw[(g, e)][:], w_view[g, :, e, :])
 
-        load_v(0)
-        load_s(0)
-        load_s(1)
-        load_v(1)
-        load_s(2)
-        load_v(2)
-        load_s(3)
-        load_v(3)
+        for t in range(PACK):
+            load_v(t)
+            load_s(t)
         for e in range(E):
             for g in range(PASSES):
                 load_w(g, e)
@@ -72,11 +67,10 @@ def tile_routed_moe_kernel(tc, xT, w, gate, offs, out):
         picked = keep.tile([P, PACK, S], F32, name="picked")
         x_grouped = {}
         w_grouped = {}
-        for e in range(E):
-            w_grouped[e] = keep.tile([P, PASSES, N, PACK], BF16, name="w_grouped%d" % e, align_bytes=64)
-            for g in range(PASSES):
-                if (g, e) != (SCALAR_PASS, 1):
-                    x_grouped[(g, e)] = keep.tile([P, C, PACK], BF16, name="x_grouped%d%d" % (g, e), align_bytes=64)
+        w_grouped[0] = keep.tile([P, PASSES, N, PACK], BF16, name="w_grouped0", align_bytes=64)
+        x_grouped[(SCALAR_PASS, 0)] = keep.tile([P, C, PACK], BF16, name="x_grouped_s0", align_bytes=64)
+        x_grouped[(VECTOR_PASS, 0)] = keep.tile([P, C, PACK], BF16, name="x_grouped_v0", tag="link_w", align_bytes=64)
+        x_grouped[(VECTOR_PASS, 1)] = keep.tile([P, C, PACK], BF16, name="x_grouped_v1", align_bytes=64)
         x_codes = {}
         x_scales = {}
         w_codes = {}
@@ -184,12 +178,15 @@ def tile_routed_moe_kernel(tc, xT, w, gate, offs, out):
         x_grouped[(SCALAR_PASS, 1)] = keep.tile([P, C, PACK], BF16, name="x_grouped_late", tag="link", align_bytes=64)
         for t in range(PACK):
             gather_scalar(t, 1)
-        for e in range(E):
-            for g in range(PASSES):
-                group_w(g, e)
+        for g in range(PASSES):
+            group_w(g, 0)
         for e in range(E):
             group_x(e)
         for e in range(E):
+            if e == 1:
+                w_grouped[1] = keep.tile([P, PASSES, N, PACK], BF16, name="w_grouped1", tag="link_w", align_bytes=64)
+                for g in range(PASSES):
+                    group_w(g, 1)
             quantize_w(e)
             quantize_x(VECTOR_PASS, e)
             multiply(VECTOR_PASS, e, True)

@@ -31,7 +31,11 @@ def tile_routed_moe_kernel(tc, xT, w, gate, offs, out):
         psum = ctx.enter_context(tc.psum_pool(name="psum", bufs=1))
 
         offsets = keep.tile([P, S // 16], U16, name="offsets")
-        nc.sync.dma_start(offsets[:], offs)
+
+        zeros = keep.tile([P, 1], F32, name="zeros")
+        nc.gpsimd.memset(zeros[:], 0.0)
+        unused = keep.tile([P, 1], F32, name="unused")
+        nc.scalar.activation(unused[:], zeros[:], COPY)
 
         x_view = xT.rearrange("(g p t) n -> g p t n", p=P, t=PACK)
         w_view = w.rearrange("e (g p j) n -> g p e (j n)", p=P, j=PACK)
@@ -56,6 +60,8 @@ def tile_routed_moe_kernel(tc, xT, w, gate, offs, out):
 
         for t in range(PACK):
             load_v(t)
+            if t == 0:
+                nc.sync.dma_start(offsets[:], offs)
             load_s(t)
         for e in range(E):
             for g in range(PASSES):
@@ -192,13 +198,8 @@ def tile_routed_moe_kernel(tc, xT, w, gate, offs, out):
             multiply(VECTOR_PASS, e, True)
             quantize_x(SCALAR_PASS, e)
             multiply(SCALAR_PASS, e, False)
-            if e == 0:
-                empty_half(0, 0)
-                empty_half(0, 1)
-            else:
-                empty_bank(1)
-        scatter_half(0, 0)
-        scatter_half(0, 1)
+            empty_bank(e)
+        scatter(0)
         scatter(1)
 
         nc.sync.dma_start(out, window[:])

@@ -77,6 +77,9 @@ def tile_routed_moe_kernel(tc, xT, w, gate, offs, out):
         x_grouped[(SCALAR_PASS, 0)] = keep.tile([P, C, PACK], BF16, name="x_grouped_s0", align_bytes=64)
         x_grouped[(VECTOR_PASS, 0)] = keep.tile([P, C, PACK], BF16, name="x_grouped_v0", tag="link_w", align_bytes=64)
         x_grouped[(VECTOR_PASS, 1)] = keep.tile([P, C, PACK], BF16, name="x_grouped_v1", align_bytes=64)
+        HALF = C // 2
+        x_half = {}
+        x_half[0] = keep.tile([P, HALF, PACK], BF16, name="x_half0", align_bytes=64)
         x_codes = {}
         x_scales = {}
         w_codes = {}
@@ -100,6 +103,10 @@ def tile_routed_moe_kernel(tc, xT, w, gate, offs, out):
         def gather_scalar(t, e):
             nc.scalar.activation(x_grouped[(SCALAR_PASS, e)][:, :, t], s_bf16[:, t, :].indirect(slots(e)), COPY)
 
+        def gather_scalar_half(t, h):
+            first = (C + h * HALF) // 16
+            nc.scalar.activation(x_half[h][:, :, t], s_bf16[:, t, :].indirect(offsets[:, first : first + HALF // 16]), COPY)
+
         def group_x(e):
             nc.vector.tensor_copy(
                 x_grouped[(VECTOR_PASS, e)][:].rearrange("p (c i) t -> p c t i", i=4),
@@ -113,6 +120,17 @@ def tile_routed_moe_kernel(tc, xT, w, gate, offs, out):
                 out=x_codes[(g, e)][:].bitcast(FP8X4),
                 scales=x_scales[(g, e)][:],
                 in_=x_grouped[(g, e)][:].rearrange("p c t -> p (c t)"),
+            )
+
+        def quantize_half(h):
+            if h == 0:
+                x_codes[(SCALAR_PASS, 1)] = keep.tile([P, C], U32, name="x_codes_s1", align_bytes=64)
+                x_scales[(SCALAR_PASS, 1)] = keep.tile([P, C], U8, name="x_scales_s1", align_bytes=64)
+            cols = slice(h * HALF, (h + 1) * HALF)
+            nc.vector.quantize_mx(
+                out=x_codes[(SCALAR_PASS, 1)][:, cols].bitcast(FP8X4),
+                scales=x_scales[(SCALAR_PASS, 1)][:, cols],
+                in_=x_half[h][:].rearrange("p c t -> p (c t)"),
             )
 
         def group_w(g, e):
@@ -149,8 +167,6 @@ def tile_routed_moe_kernel(tc, xT, w, gate, offs, out):
         window = keep.tile([P, T], F32, name="window")
         sums_sb = {}
 
-        HALF = C // 2
-
         def empty_half(e, h):
             sums_sb[(e, h)] = keep.tile([P, HALF], F32, name="sums_sb%d%d" % (e, h))
             if h == 0:
@@ -179,11 +195,12 @@ def tile_routed_moe_kernel(tc, xT, w, gate, offs, out):
         for t in range(PACK):
             cast_plane(t)
             gather_scalar(t, 0)
+            gather_scalar_half(t, 0)
             if t > 0:
                 gather_all(t)
-        x_grouped[(SCALAR_PASS, 1)] = keep.tile([P, C, PACK], BF16, name="x_grouped_late", tag="link", align_bytes=64)
+        x_half[1] = keep.tile([P, HALF, PACK], BF16, name="x_half_late", tag="link", align_bytes=64)
         for t in range(PACK):
-            gather_scalar(t, 1)
+            gather_scalar_half(t, 1)
         for g in range(PASSES):
             group_w(g, 0)
         for e in range(E):
@@ -196,7 +213,11 @@ def tile_routed_moe_kernel(tc, xT, w, gate, offs, out):
             quantize_w(e)
             quantize_x(VECTOR_PASS, e)
             multiply(VECTOR_PASS, e, True)
-            quantize_x(SCALAR_PASS, e)
+            if e == 0:
+                quantize_x(SCALAR_PASS, e)
+            else:
+                quantize_half(0)
+                quantize_half(1)
             multiply(SCALAR_PASS, e, False)
             empty_bank(e)
         scatter(0)

from contextlib import ExitStack

import concourse.mybir as mybir

K, T, E, C, N = 1024, 512, 2, 256, 128
FLOPS = 2 * K * N * E * C

F32 = mybir.dt.float32
BF16 = mybir.dt.bfloat16
U32 = mybir.dt.uint32
U16 = mybir.dt.uint16
U8 = mybir.dt.uint8
FP8X4 = mybir.dt.float8_e4m3fn_x4
MULT = mybir.AluOpType.mult
COPY = mybir.ActivationFunctionType.Copy

P = 128
PACK = 4
K_PASS = P * PACK
PASSES = K // K_PASS
S = E * C
LIST_COLS = C // 16
SCALAR_PASS = 0
VECTOR_PASS = 1


def tile_routed_moe_kernel(tc, xT, w, gate, offs, out):
    nc = tc.nc
    with ExitStack() as ctx:
        keep = ctx.enter_context(tc.tile_pool(name="keep", bufs=1))
        psum = ctx.enter_context(tc.psum_pool(name="psum", bufs=1))

        offsets = keep.tile([P, S // 16], U16, name="offsets")

        zeros = keep.tile([P, 1], F32, name="zeros")
        nc.gpsimd.memset(zeros[:], 0.0)
        unused = keep.tile([P, 1], F32, name="unused")
        nc.scalar.activation(unused[:], zeros[:], COPY)

        x_view = xT.rearrange("(g p t) n -> g p t n", p=P, t=PACK)
        w_view = w.rearrange("e (g p j) n -> g p e (j n)", p=P, j=PACK)

        v_raw = keep.tile([P, PACK * T], F32, name="v_raw")
        s_raw = {}
        w_raw = {}

        def v_cols(t, planes=1):
            return slice((PACK - 1 - t) * T, (PACK - 1 - t + planes) * T)

        def load_v(t):
            nc.sync.dma_start(v_raw[:, v_cols(t)], x_view[VECTOR_PASS, :, t, :])

        def load_s(t):
            s_raw[t] = keep.tile([P, T], F32, name="s_raw%d" % t, tag="link" if t == PACK - 1 else "s_raw%d" % t, align_bytes=64)
            nc.sync.dma_start(s_raw[t][:], x_view[SCALAR_PASS, :, t, :])

        def load_w(g, e):
            w_raw[(g, e)] = keep.tile([P, PACK * N], F32, name="w_raw%d%d" % (g, e))
            nc.sync.dma_start(w_raw[(g, e)][:], w_view[g, :, e, :])

        for t in range(PACK):
            load_v(t)
            if t == 0:
                nc.sync.dma_start(offsets[:], offs)
            load_s(t)
        for e in range(E):
            for g in range(PASSES):
                load_w(g, e)
        gate_sb = keep.tile([P, S], F32, name="gate_sb")
        nc.sync.dma_start(gate_sb[:], gate)

        s_bf16 = keep.tile([P, PACK, T], BF16, name="s_bf16")
        picked = keep.tile([P, PACK, S], F32, name="picked")
        x_grouped = {}
        w_grouped = {}
        w_grouped[0] = keep.tile([P, PASSES, N, PACK], BF16, name="w_grouped0", align_bytes=64)
        x_grouped[(SCALAR_PASS, 0)] = keep.tile([P, C, PACK], BF16, name="x_grouped_s0", align_bytes=64)
        x_grouped[(VECTOR_PASS, 0)] = keep.tile([P, C, PACK], BF16, name="x_grouped_v0", tag="link_w", align_bytes=64)
        x_grouped[(VECTOR_PASS, 1)] = keep.tile([P, C, PACK], BF16, name="x_grouped_v1", align_bytes=64)
        HALF = C // 2
        x_half = {}
        x_half[0] = keep.tile([P, HALF, PACK], BF16, name="x_half0", align_bytes=64)
        x_codes = {}
        x_scales = {}
        w_codes = {}
        w_scales = {}

        def slots(e):
            return offsets[:, e * LIST_COLS : (e + 1) * LIST_COLS]

        def of_expert(e):
            return slice(e * C, (e + 1) * C)

        def gather_half(t, e):
            nc.vector.tensor_copy(picked[:, t, of_expert(e)], v_raw[:, v_cols(t)].indirect(slots(e)))

        def gather_all(t):
            nc.vector.tensor_copy(picked[:, t, :], v_raw[:, v_cols(t, 2)].indirect(offsets[:]))

        def cast_plane(t):
            nc.gpsimd.tensor_copy(s_bf16[:, t, :], s_raw[t][:])

        def gather_scalar(t, e):
            nc.scalar.activation(x_grouped[(SCALAR_PASS, e)][:, :, t], s_bf16[:, t, :].indirect(slots(e)), COPY)

        def gather_scalar_half(t, h):
            first = (C + h * HALF) // 16
            nc.scalar.activation(x_half[h][:, :, t], s_bf16[:, t, :].indirect(offsets[:, first : first + HALF // 16]), COPY)

        def group_x(e):
            nc.vector.tensor_copy(
                x_grouped[(VECTOR_PASS, e)][:].rearrange("p (c i) t -> p c t i", i=4),
                picked[:, :, of_expert(e)].rearrange("p t (c i) -> p c t i", i=4),
            )

        def quantize_x(g, e):
            x_codes[(g, e)] = keep.tile([P, C], U32, name="x_codes%d%d" % (g, e), align_bytes=64)
            x_scales[(g, e)] = keep.tile([P, C], U8, name="x_scales%d%d" % (g, e), align_bytes=64)
            nc.vector.quantize_mx(
                out=x_codes[(g, e)][:].bitcast(FP8X4),
                scales=x_scales[(g, e)][:],
                in_=x_grouped[(g, e)][:].rearrange("p c t -> p (c t)"),
            )

        def quantize_half(h):
            if h == 0:
                x_codes[(SCALAR_PASS, 1)] = keep.tile([P, C], U32, name="x_codes_s1", align_bytes=64)
                x_scales[(SCALAR_PASS, 1)] = keep.tile([P, C], U8, name="x_scales_s1", align_bytes=64)
            cols = slice(h * HALF, (h + 1) * HALF)
            nc.vector.quantize_mx(
                out=x_codes[(SCALAR_PASS, 1)][:, cols].bitcast(FP8X4),
                scales=x_scales[(SCALAR_PASS, 1)][:, cols],
                in_=x_half[h][:].rearrange("p c t -> p (c t)"),
            )

        def group_w(g, e):
            nc.vector.tensor_copy(
                w_grouped[e][:, g, :, :].rearrange("p (c i) j -> p c j i", i=4),
                w_raw[(g, e)][:].rearrange("p (j c i) -> p c j i", j=PACK, i=4),
            )

        def quantize_w(e):
            w_codes[e] = keep.tile([P, PASSES * N], U32, name="w_codes%d" % e, align_bytes=64)
            w_scales[e] = keep.tile([P, PASSES * N], U8, name="w_scales%d" % e, align_bytes=64)
            nc.vector.quantize_mx(
                out=w_codes[e][:].bitcast(FP8X4),
                scales=w_scales[e][:],
                in_=w_grouped[e][:].rearrange("p g n j -> p (g n j)"),
            )

        sums = {}
        for e in range(E):
            sums[e] = psum.tile([P, C], F32, name="sums%d" % e)

        def multiply(g, e, first):
            w_cols = slice(g * N, (g + 1) * N)
            nc.tensor.matmul_mx(
                out=sums[e][:],
                lhsT=w_codes[e][:, w_cols].bitcast(FP8X4),
                lhsT_scale=w_scales[e][:, w_cols],
                rhs=x_codes[(g, e)][:].bitcast(FP8X4),
                rhs_scale=x_scales[(g, e)][:],
                start=first,
                stop=not first,
            )

        window = keep.tile([P, T], F32, name="window")
        sums_sb = {}

        def empty_half(e, h):
            sums_sb[(e, h)] = keep.tile([P, HALF], F32, name="sums_sb%d%d" % (e, h))
            if h == 0:
                nc.vector.tensor_copy(sums_sb[(e, h)][:], sums[e][:, 0:HALF])
            else:
                nc.scalar.copy(sums_sb[(e, h)][:], sums[e][:, HALF:C])

        def scatter_half(e, h):
            first = e * C + h * HALF
            nc.vector.tensor_tensor(
                window[:].indirect(offsets[:, first // 16 : (first + HALF) // 16]),
                sums_sb[(e, h)][:],
                gate_sb[:, first : first + HALF],
                MULT,
            )

        def empty_bank(e):
            sums_sb[e] = keep.tile([P, C], F32, name="sums_sb%d" % e)
            nc.scalar.copy(sums_sb[e][:], sums[e][:])

        def scatter(e):
            nc.vector.tensor_tensor(window[:].indirect(slots(e)), sums_sb[e][:], gate_sb[:, of_expert(e)], MULT)

        gather_half(0, 0)
        gather_half(0, 1)
        for t in range(PACK):
            cast_plane(t)
            gather_scalar(t, 0)
            gather_scalar_half(t, 0)
            if t > 0:
                gather_all(t)
        x_half[1] = keep.tile([P, HALF, PACK], BF16, name="x_half_late", tag="link", align_bytes=64)
        for t in range(PACK):
            gather_scalar_half(t, 1)
        for g in range(PASSES):
            group_w(g, 0)
        for e in range(E):
            group_x(e)
        for e in range(E):
            if e == 1:
                w_grouped[1] = keep.tile([P, PASSES, N, PACK], BF16, name="w_grouped1", tag="link_w", align_bytes=64)
                for g in range(PASSES):
                    group_w(g, 1)
            quantize_w(e)
            quantize_x(VECTOR_PASS, e)
            multiply(VECTOR_PASS, e, True)
            if e == 0:
                quantize_x(SCALAR_PASS, e)
            else:
                quantize_half(0)
                quantize_half(1)
            multiply(SCALAR_PASS, e, False)
            empty_bank(e)
        scatter(0)
        scatter(1)

        nc.sync.dma_start(out, window[:])
